import numpy as np, ml_dtypes
CORES = [61,69,101,62,70,102]
N = 6
import mx_ref
NC = 256
BF = ml_dtypes.bfloat16
def setup_inputs(rng):
    def f(*shape):
        return mx_ref.flush((rng.standard_normal(shape, dtype=np.float32) * np.exp2(rng.integers(-2, 3, shape[:-1] + (1,)))).astype(BF))
    return {"w": f(N, 128, N * 512), "x": f(N, 128, 4 * NC)}
def setup_inputs_blocks(rng):
    d = setup_inputs(rng)
    for k in ("w", "x"): d[k] = mx_ref.spread(d[k], rng, 2)
    return d
def setup_inputs_wide(rng):
    d = setup_inputs(rng)
    for k in ("w", "x"): d[k] = mx_ref.flush((d[k].astype(np.float32) * np.exp2(rng.integers(-8, 9, (N, 1, 1))).astype(np.float32)).astype(BF))
    return d
def setup_inputs_zeros(rng):
    d = setup_inputs(rng); v = d["x"].reshape(N, 128, -1, 4).copy()
    v[np.broadcast_to((rng.random((N, 1, v.shape[2], 1)) < 0.33), v.shape)] = 0
    d["x"] = v.reshape(d["x"].shape)
    return d
def reference(w, x):
    QX = [mx_ref.quantize(x[j]) for j in range(N)]
    y = np.zeros((N, 128, NC), np.float32)
    for r in range(N):
        for j in range(N):
            p = mx_ref.matmul(mx_ref.quantize(w[r][:, 512 * j:512 * j + 512]), QX[j])
            y[r] = p if j == 0 else y[r] + p
    return {"y": y}

@@ -1,0 +1,139 @@
+from concourse.bass import DstId, RemoteDMATransfer
+from concourse.mybir import dt
+
+N = 6
+NC = 256
+WC = 128
+
+SCRATCH = {
+    "xb": ("sbuf", [128, 4 * NC], "bfloat16"),
+    "wb": ("sbuf", [128, N * 4 * WC], "bfloat16"),
+    "xq": ("sbuf", [128, N * NC], "float8_e4m3fn_x4"),
+    "xs": ("sbuf", [128, N * NC], "uint8"),
+    "wq": ("sbuf", [128, N * WC], "float8_e4m3fn_x4"),
+    "ws": ("sbuf", [128, N * WC], "uint8"),
+    "acc": ("psum", [128, 512], "float32"),
+    "yb": ("sbuf", [128, NC], "float32"),
+}
+SEMAPHORES = ["ldx", "ldw", "qx", "qw", "mm", "cp", "st", "sent"] + ["arr%d" % k for k in range(N)]
+
+
+def _bits(m):
+    return [e for e in range(m.bit_length()) if (m >> e) & 1]
+
+
+def _plan(cores, topo):
+    chips = sorted({topo.chip(c) for c in cores})
+    lone = [a for a in chips if not any(topo.same_plane(a, b) for b in chips if b != a)][0]
+    twins = [a for a in chips if a != lone]
+
+    def split(ch):
+        here = [c for c in cores if topo.chip(c) == ch]
+        away = [c for c in cores if topo.chip(c) != ch]
+        gate = [c for c in here if all(topo.may_write(c, d) for d in away)][0]
+        return [c for c in here if c != gate][0], gate
+
+    pn, po = split(lone)
+    qn, qo = split(twins[0])
+    rn, ro = split(twins[1])
+    slot = {pn: 0, po: 1, qn: 2, qo: 3, ro: 4, rn: 5}
+    mate_of = {pn: po, po: pn, qn: qo, qo: qn, rn: ro, ro: rn}
+
+    def eng(src, key):
+        wide = _bits(topo.mask(src, mate_of[src]))
+        far = _bits(topo.mask(src, [c for c in cores if topo.chip(c) != topo.chip(src)][0]))
+        h = len(far) // 2
+        return {"wide": wide, "far": far, "far0": far[:h], "far1": far[h:],
+                "near": [e for e in wide if e not in far]}[key]
+
+    raw = {
+        pn: [((), 0, 1, [(po, "near")]),
+             ((3, 4), 3, 2, [(po, "wide")]),
+             ((2,), 2, 1, [(po, "wide")])],
+        po: [((), 1, 1, [(qo, "far0"), (ro, "far1")]),
+             ((), 1, 1, [(pn, "near")]),
+             ((0,), 0, 1, [(qn, "far0"), (rn, "far1")]),
+             ((5,), 5, 1, [(pn, "wide")])],
+        qn: [((), 2, 1, [(qo, "near")]),
+             ((), 2, 1, [(rn, "far")]),
+             ((4, 5), 4, 2, [(qo, "wide")]),
+             ((0,), 0, 1, [(qo, "wide")])],
+        rn: [((), 5, 1, [(ro, "near")]),
+             ((), 5, 1, [(qn, "far")]),
+             ((2, 3), 2, 2, [(ro, "wide")]),
+             ((0,), 0, 1, [(ro, "wide")])],
+        qo: [((), 3, 1, [(pn, "far0"), (rn, "far1")]),
+             ((), 3, 1, [(qn, "near")]),
+             ((2,), 2, 1, [(pn, "far")]),
+             ((1,), 1, 1, [(qn, "wide")])],
+        ro: [((), 4, 1, [(pn, "far0"), (qn, "far1")]),
+             ((), 4, 1, [(rn, "near")]),
+             ((5,), 5, 1, [(po, "far")]),
+             ((1,), 1, 1, [(rn, "wide")])],
+    }
+    sends = {c: [(need, lo, n, [(d, eng(c, k)) for d, k in tg]) for need, lo, n, tg in raw[c]] for c in raw}
+    order = {pn: (0, 1, 3, 4, 2, 5), po: (1, 0, 3, 4, 5, 2),
+             qn: (2, 3, 5, 4, 1, 0), qo: (3, 2, 1, 4, 5, 0),
+             rn: (5, 4, 2, 3, 1, 0), ro: (4, 5, 1, 2, 3, 0)}
+    return slot, sends, order
+
+
+def rank_program(g, core, T, topo):
+    rank = T.rank_of(core)
+    if rank is None:
+        return
+    cores = list(T.cores)
+    slot, sends, order = _plan(cores, topo)
+    mine = slot[core]
+    rank_in = {slot[c]: T.rank_of(c) for c in cores}
+
+    lands = {}
+    for c in cores:
+        for need, lo, n, targets in sends[c]:
+            for d, e in targets:
+                if d == core:
+                    for s in range(lo, lo + n):
+                        lands[s] = (T.sem["arr%d" % lo], 2 * len(e))
+
+    g.sync.dma_start(T.xb[:], T.x[:]).then_inc(T.sem.ldx, 16)
+    g.sync.dma_start(T.wb[:], T.w[:]).then_inc(T.sem.ldw, 16)
+
+    g.vector.wait_ge(T.sem.ldx, 16)
+    g.vector.quantize_mx(T.xq[:, mine * NC:(mine + 1) * NC], T.xs[:, mine * NC:(mine + 1) * NC],
+                         T.xb[:]).then_inc(T.sem.qx, 1)
+    g.vector.wait_ge(T.sem.ldw, 16)
+    for j in range(N):
+        g.vector.quantize_mx(T.wq[:, j * WC:(j + 1) * WC], T.ws[:, j * WC:(j + 1) * WC],
+                             T.wb[:, j * 4 * WC:(j + 1) * 4 * WC]).then_inc(T.sem.qw, 1)
+
+    left = 0
+    g.wait_ge(T.sem.qx, 1)
+    for need, lo, n, targets in sends[core]:
+        for s in need:
+            g.wait_ge(lands[s][0], lands[s][1])
+        a, b = lo * NC, (lo + n) * NC
+        for ap in (T.xq[:, a:b].bitcast(dt.uint8), T.xs[:, a:b]):
+            trs = []
+            for d, e in targets:
+                rid, pid, _se = topo.addr(d)
+                trs.append(RemoteDMATransfer(dst_ids=[DstId(rid=rid, pnc=pid)], dma_engine_mask=sum(1 << k for k in e),
+                                             remote_sem=T.sem["arr%d" % lo], src=ap, dst=ap))
+                left += len(e)
+            g.remote_dma_fused(trs, local_sem=T.sem.sent)
+
+    g.tensor.wait_ge(T.sem.qx, 1)
+    g.tensor.wait_ge(T.sem.qw, N)
+    for i, s in enumerate(order[core]):
+        if s != mine:
+            g.tensor.wait_ge(lands[s][0], lands[s][1])
+        j = rank_in[s]
+        mmi = g.tensor.matmul_mx(T.acc[:, 0:NC], T.wq[:, j * WC:(j + 1) * WC], T.ws[:, j * WC:(j + 1) * WC],
+                                 T.xq[:, s * NC:(s + 1) * NC], T.xs[:, s * NC:(s + 1) * NC], i == 0, i == N - 1)
+    mmi.then_inc(T.sem.mm, 1)
+
+    g.vector.wait_ge(T.sem.mm, 1)
+    g.vector.tensor_copy(T.yb[:], T.acc[:, 0:NC]).then_inc(T.sem.cp, 1)
+    g.sync.wait_ge(T.sem.cp, 1)
+    g.sync.dma_start(T.y[:], T.yb[:]).then_inc(T.sem.st, 16)
+    g.sync.wait_ge(T.sem.st, 16)
+    g.wait_ge(T.sem.sent, left)

@@ -4,6 +4,7 @@ from concourse.mybir import dt
 N = 6
 NC = 256
 WC = 128
+SIM = 112
 
 SCRATCH = {
     "xb": ("sbuf", [128, 4 * NC], "bfloat16"),
@@ -15,7 +16,8 @@ SCRATCH = {
     "acc": ("psum", [128, 512], "float32"),
     "yb": ("sbuf", [128, NC], "float32"),
 }
-SEMAPHORES = ["ldx", "ldw", "qx", "qw", "mm", "cp", "st", "sent"] + ["arr%d" % k for k in range(N)]
+SEMAPHORES = (["ldx", "ldw", "qx", "qw", "mm", "cp", "st", "sent"]
+              + ["as%d" % k for k in range(N)] + ["ac%d" % k for k in range(N)])
 
 
 def _bits(m):
@@ -33,11 +35,16 @@ def _plan(cores, topo):
         gate = [c for c in here if all(topo.may_write(c, d) for d in away)][0]
         return [c for c in here if c != gate][0], gate
 
+    def carrier(gate):
+        return [c for c in range(SIM) if c not in cores and topo.chip(c) == topo.chip(gate)
+                and topo.die(c) != topo.die(gate) and all(topo.may_write(c, d) for d in cores)][0]
+
     pn, po = split(lone)
     qn, qo = split(twins[0])
     rn, ro = split(twins[1])
+    hp, hq = carrier(po), carrier(qo)
     slot = {pn: 0, po: 1, qn: 2, qo: 3, ro: 4, rn: 5}
-    mate_of = {pn: po, po: pn, qn: qo, qo: qn, rn: ro, ro: rn}
+    mate_of = {pn: po, po: pn, qn: qo, qo: qn, rn: ro, ro: rn, hp: po, hq: qo}
 
     def eng(src, key):
         wide = _bits(topo.mask(src, mate_of[src]))
@@ -47,93 +54,99 @@ def _plan(cores, topo):
                 "near": [e for e in wide if e not in far]}[key]
 
     raw = {
-        pn: [((), 0, 1, [(po, "near")]),
-             ((3, 4), 3, 2, [(po, "wide")]),
+        pn: [((), 0, 1, [(hp, "near")]),
+             ((), 0, 1, [(po, "far")]),
+             ((3,), 3, 1, [(po, "wide")]),
              ((2,), 2, 1, [(po, "wide")])],
+        hp: [((0,), 0, 1, [(qn, "far0"), (rn, "far1")])],
         po: [((), 1, 1, [(qo, "far0"), (ro, "far1")]),
              ((), 1, 1, [(pn, "near")]),
-             ((0,), 0, 1, [(qn, "far0"), (rn, "far1")]),
+             ((4,), 4, 1, [(pn, "wide")]),
              ((5,), 5, 1, [(pn, "wide")])],
-        qn: [((), 2, 1, [(qo, "near")]),
-             ((), 2, 1, [(rn, "far")]),
-             ((4, 5), 4, 2, [(qo, "wide")]),
+        qn: [((), 2, 1, [(rn, "far"), (hq, "near")]),
+             ((), 2, 1, [(qo, "near")]),
+             ((4,), 4, 1, [(qo, "wide")]),
              ((0,), 0, 1, [(qo, "wide")])],
-        rn: [((), 5, 1, [(ro, "near")]),
-             ((), 5, 1, [(qn, "far")]),
-             ((2, 3), 2, 2, [(ro, "wide")]),
-             ((0,), 0, 1, [(ro, "wide")])],
+        hq: [((2,), 2, 1, [(pn, "far")])],
         qo: [((), 3, 1, [(pn, "far0"), (rn, "far1")]),
              ((), 3, 1, [(qn, "near")]),
-             ((2,), 2, 1, [(pn, "far")]),
+             ((5,), 5, 1, [(qn, "wide")]),
              ((1,), 1, 1, [(qn, "wide")])],
-        ro: [((), 4, 1, [(pn, "far0"), (qn, "far1")]),
+        rn: [((), 5, 1, [(qo, "far"), (ro, "near")]),
+             ((2,), 2, 1, [(ro, "wide")]),
+             ((3,), 3, 1, [(ro, "wide")]),
+             ((0,), 0, 1, [(ro, "wide")])],
+        ro: [((), 4, 1, [(po, "far0"), (qn, "far1")]),
              ((), 4, 1, [(rn, "near")]),
              ((5,), 5, 1, [(po, "far")]),
              ((1,), 1, 1, [(rn, "wide")])],
     }
     sends = {c: [(need, lo, n, [(d, eng(c, k)) for d, k in tg]) for need, lo, n, tg in raw[c]] for c in raw}
-    order = {pn: (0, 1, 3, 4, 2, 5), po: (1, 0, 3, 4, 5, 2),
-             qn: (2, 3, 5, 4, 1, 0), qo: (3, 2, 1, 4, 5, 0),
-             rn: (5, 4, 2, 3, 1, 0), ro: (4, 5, 1, 2, 3, 0)}
+    order = {pn: (0, 1, 3, 4, 2, 5), po: (1, 0, 4, 3, 5, 2),
+             qn: (2, 3, 5, 4, 0, 1), qo: (3, 2, 5, 4, 1, 0),
+             rn: (5, 4, 2, 3, 0, 1), ro: (4, 5, 2, 3, 1, 0)}
     return slot, sends, order
 
 
 def rank_program(g, core, T, topo):
     rank = T.rank_of(core)
-    if rank is None:
-        return
     cores = list(T.cores)
     slot, sends, order = _plan(cores, topo)
-    mine = slot[core]
+    if core not in sends:
+        return
     rank_in = {slot[c]: T.rank_of(c) for c in cores}
 
     lands = {}
-    for c in cores:
+    for c in sends:
         for need, lo, n, targets in sends[c]:
             for d, e in targets:
                 if d == core:
                     for s in range(lo, lo + n):
-                        lands[s] = (T.sem["arr%d" % lo], 2 * len(e))
+                        lands[s] = (lo, len(e))
 
-    g.sync.dma_start(T.xb[:], T.x[:]).then_inc(T.sem.ldx, 16)
-    g.sync.dma_start(T.wb[:], T.w[:]).then_inc(T.sem.ldw, 16)
+    if rank is not None:
+        mine = slot[core]
+        g.sync.dma_start(T.xb[:], T.x[:]).then_inc(T.sem.ldx, 16)
+        g.sync.dma_start(T.wb[:], T.w[:]).then_inc(T.sem.ldw, 16)
 
-    g.vector.wait_ge(T.sem.ldx, 16)
-    g.vector.quantize_mx(T.xq[:, mine * NC:(mine + 1) * NC], T.xs[:, mine * NC:(mine + 1) * NC],
-                         T.xb[:]).then_inc(T.sem.qx, 1)
-    g.vector.wait_ge(T.sem.ldw, 16)
-    for j in range(N):
-        g.vector.quantize_mx(T.wq[:, j * WC:(j + 1) * WC], T.ws[:, j * WC:(j + 1) * WC],
-                             T.wb[:, j * 4 * WC:(j + 1) * 4 * WC]).then_inc(T.sem.qw, 1)
+        g.vector.wait_ge(T.sem.ldx, 16)
+        g.vector.quantize_mx(T.xq[:, mine * NC:(mine + 1) * NC], T.xs[:, mine * NC:(mine + 1) * NC],
+                             T.xb[:]).then_inc(T.sem.qx, 1)
+        g.vector.wait_ge(T.sem.ldw, 16)
+        for j in range(N):
+            g.vector.quantize_mx(T.wq[:, j * WC:(j + 1) * WC], T.ws[:, j * WC:(j + 1) * WC],
+                                 T.wb[:, j * 4 * WC:(j + 1) * 4 * WC]).then_inc(T.sem.qw, 1)
+        g.wait_ge(T.sem.qx, 1)
 
     left = 0
-    g.wait_ge(T.sem.qx, 1)
     for need, lo, n, targets in sends[core]:
-        for s in need:
-            g.wait_ge(lands[s][0], lands[s][1])
         a, b = lo * NC, (lo + n) * NC
-        for ap in (T.xq[:, a:b].bitcast(dt.uint8), T.xs[:, a:b]):
+        for tag, ap in (("as%d", T.xs[:, a:b]), ("ac%d", T.xq[:, a:b].bitcast(dt.uint8))):
+            for s in need:
+                g.wait_ge(T.sem[tag % lands[s][0]], lands[s][1])
             trs = []
             for d, e in targets:
                 rid, pid, _se = topo.addr(d)
                 trs.append(RemoteDMATransfer(dst_ids=[DstId(rid=rid, pnc=pid)], dma_engine_mask=sum(1 << k for k in e),
-                                             remote_sem=T.sem["arr%d" % lo], src=ap, dst=ap))
+                                             remote_sem=T.sem[tag % lo], src=ap, dst=ap))
                 left += len(e)
             g.remote_dma_fused(trs, local_sem=T.sem.sent)
 
-    g.tensor.wait_ge(T.sem.qx, 1)
-    g.tensor.wait_ge(T.sem.qw, N)
-    for i, s in enumerate(order[core]):
-        if s != mine:
-            g.tensor.wait_ge(lands[s][0], lands[s][1])
-        j = rank_in[s]
-        mmi = g.tensor.matmul_mx(T.acc[:, 0:NC], T.wq[:, j * WC:(j + 1) * WC], T.ws[:, j * WC:(j + 1) * WC],
-                                 T.xq[:, s * NC:(s + 1) * NC], T.xs[:, s * NC:(s + 1) * NC], i == 0, i == N - 1)
-    mmi.then_inc(T.sem.mm, 1)
+    if rank is not None:
+        g.tensor.wait_ge(T.sem.qx, 1)
+        g.tensor.wait_ge(T.sem.qw, N)
+        for i, s in enumerate(order[core]):
+            if s != mine:
+                g.tensor.wait_ge(T.sem["as%d" % lands[s][0]], lands[s][1])
+                g.tensor.wait_ge(T.sem["ac%d" % lands[s][0]], lands[s][1])
+            j = rank_in[s]
+            mmi = g.tensor.matmul_mx(T.acc[:, 0:NC], T.wq[:, j * WC:(j + 1) * WC], T.ws[:, j * WC:(j + 1) * WC],
+                                     T.xq[:, s * NC:(s + 1) * NC], T.xs[:, s * NC:(s + 1) * NC], i == 0, i == N - 1)
+        mmi.then_inc(T.sem.mm, 1)
 
-    g.vector.wait_ge(T.sem.mm, 1)
-    g.vector.tensor_copy(T.yb[:], T.acc[:, 0:NC]).then_inc(T.sem.cp, 1)
-    g.sync.wait_ge(T.sem.cp, 1)
-    g.sync.dma_start(T.y[:], T.yb[:]).then_inc(T.sem.st, 16)
-    g.sync.wait_ge(T.sem.st, 16)
+        g.vector.wait_ge(T.sem.mm, 1)
+        g.vector.tensor_copy(T.yb[:], T.acc[:, 0:NC]).then_inc(T.sem.cp, 1)
+        g.sync.wait_ge(T.sem.cp, 1)
+        g.sync.dma_start(T.y[:], T.yb[:]).then_inc(T.sem.st, 16)
+        g.sync.wait_ge(T.sem.st, 16)
     g.wait_ge(T.sem.sent, left)

@@ -3,7 +3,9 @@ from concourse.mybir import dt
 
 N = 6
 NC = 256
+U = 128
 WC = 128
+BANK = 512
 SIM = 112
 
 SCRATCH = {
@@ -13,11 +15,12 @@ SCRATCH = {
     "xs": ("sbuf", [128, N * NC], "uint8"),
     "wq": ("sbuf", [128, N * WC], "float8_e4m3fn_x4"),
     "ws": ("sbuf", [128, N * WC], "uint8"),
-    "acc": ("psum", [128, 512], "float32"),
+    "acc": ("psum", [128, 2 * BANK], "float32"),
     "yb": ("sbuf", [128, NC], "float32"),
 }
-SEMAPHORES = (["ldx", "ldw", "qx", "qw", "mm", "cp", "st", "sent"]
-              + ["as%d" % k for k in range(N)] + ["ac%d" % k for k in range(N)])
+PARTS = ("ca%d", "as%d", "cb%d")
+SEMAPHORES = (["lda", "ldb", "ldw", "qa", "qb", "qw", "ma", "mb", "cp", "st", "sent"]
+              + [p % k for p in PARTS for k in range(N)])
 
 
 def _bits(m):
@@ -35,16 +38,17 @@ def _plan(cores, topo):
         gate = [c for c in here if all(topo.may_write(c, d) for d in away)][0]
         return [c for c in here if c != gate][0], gate
 
-    def carrier(gate):
+    def carriers(gate, same_die):
         return [c for c in range(SIM) if c not in cores and topo.chip(c) == topo.chip(gate)
-                and topo.die(c) != topo.die(gate) and all(topo.may_write(c, d) for d in cores)][0]
+                and (topo.die(c) == topo.die(gate)) == same_die and all(topo.may_write(c, d) for d in cores)]
 
     pn, po = split(lone)
     qn, qo = split(twins[0])
     rn, ro = split(twins[1])
-    hp, hq = carrier(po), carrier(qo)
+    hp, hp2 = carriers(po, False)[:2]
+    hq, hr = carriers(qo, False)[0], carriers(ro, True)[0]
     slot = {pn: 0, po: 1, qn: 2, qo: 3, ro: 4, rn: 5}
-    mate_of = {pn: po, po: pn, qn: qo, qo: qn, rn: ro, ro: rn, hp: po, hq: qo}
+    mate_of = {pn: po, po: pn, qn: qo, qo: qn, rn: ro, ro: rn, hp: po, hp2: po, hq: qo, hr: ro}
 
     def eng(src, key):
         wide = _bits(topo.mask(src, mate_of[src]))
@@ -54,34 +58,37 @@ def _plan(cores, topo):
                 "near": [e for e in wide if e not in far]}[key]
 
     raw = {
-        pn: [((), 0, 1, [(hp, "near")]),
-             ((), 0, 1, [(po, "far")]),
-             ((3,), 3, 1, [(po, "wide")]),
-             ((2,), 2, 1, [(po, "wide")])],
-        hp: [((0,), 0, 1, [(qn, "far0"), (rn, "far1")])],
-        po: [((), 1, 1, [(qo, "far0"), (ro, "far1")]),
-             ((), 1, 1, [(pn, "near")]),
-             ((4,), 4, 1, [(pn, "wide")]),
-             ((5,), 5, 1, [(pn, "wide")])],
-        qn: [((), 2, 1, [(rn, "far"), (hq, "near")]),
-             ((), 2, 1, [(qo, "near")]),
-             ((4,), 4, 1, [(qo, "wide")]),
-             ((0,), 0, 1, [(qo, "wide")])],
-        hq: [((2,), 2, 1, [(pn, "far")])],
-        qo: [((), 3, 1, [(pn, "far0"), (rn, "far1")]),
-             ((), 3, 1, [(qn, "near")]),
-             ((5,), 5, 1, [(qn, "wide")]),
-             ((1,), 1, 1, [(qn, "wide")])],
-        rn: [((), 5, 1, [(qo, "far"), (ro, "near")]),
-             ((2,), 2, 1, [(ro, "wide")]),
-             ((3,), 3, 1, [(ro, "wide")]),
-             ((0,), 0, 1, [(ro, "wide")])],
-        ro: [((), 4, 1, [(po, "far0"), (qn, "far1")]),
-             ((), 4, 1, [(rn, "near")]),
-             ((5,), 5, 1, [(po, "far")]),
-             ((1,), 1, 1, [(rn, "wide")])],
+        pn: [(None, 0, [[(hp, "near")], [(hp2, "far")]]),
+             (None, 0, [[(po, "near")]]),
+             (3, 3, [[(po, "wide")]]),
+             (2, 2, [[(po, "wide")]])],
+        hp: [(0, 0, [[(qn, "far")]])],
+        hp2: [(0, 0, [[(rn, "far")]])],
+        po: [(None, 1, [[(qo, "far0"), (ro, "far1")]]),
+             (None, 1, [[(pn, "near")]]),
+             (4, 4, [[(pn, "wide")]]),
+             (5, 5, [[(pn, "wide")]])],
+        qn: [(None, 2, [[(hq, "near")], [(ro, "far")]]),
+             (None, 2, [[(qo, "near")]]),
+             (4, 4, [[(qo, "wide")]]),
+             (0, 0, [[(qo, "wide")]])],
+        rn: [(None, 5, [[(hr, "near")], [(qo, "far")]]),
+             (None, 5, [[(ro, "near")]]),
+             (3, 3, [[(ro, "wide")]]),
+             (0, 0, [[(ro, "wide")]])],
+        hq: [(2, 2, [[(pn, "far")]])],
+        hr: [(5, 5, [[(po, "far")]])],
+        qo: [(None, 3, [[(pn, "far0"), (rn, "far1")]]),
+             (None, 3, [[(qn, "near")]]),
+             (5, 5, [[(qn, "wide")]]),
+             (1, 1, [[(qn, "wide")]])],
+        ro: [(None, 4, [[(po, "far0"), (qn, "far1")]]),
+             (None, 4, [[(rn, "near")]]),
+             (2, 2, [[(rn, "wide")]]),
+             (1, 1, [[(rn, "wide")]])],
     }
-    sends = {c: [(need, lo, n, [(d, eng(c, k)) for d, k in tg]) for need, lo, n, tg in raw[c]] for c in raw}
+    sends = {c: [(need, s, [[(d, eng(c, k)) for d, k in call] for call in calls])
+                 for need, s, calls in raw[c]] for c in raw}
     order = {pn: (0, 1, 3, 4, 2, 5), po: (1, 0, 4, 3, 5, 2),
              qn: (2, 3, 5, 4, 0, 1), qo: (3, 2, 5, 4, 1, 0),
              rn: (5, 4, 2, 3, 0, 1), ro: (4, 5, 2, 3, 1, 0)}
@@ -98,55 +105,77 @@ def rank_program(g, core, T, topo):
 
     lands = {}
     for c in sends:
-        for need, lo, n, targets in sends[c]:
-            for d, e in targets:
-                if d == core:
-                    for s in range(lo, lo + n):
-                        lands[s] = (lo, len(e))
+        for need, s, calls in sends[c]:
+            for call in calls:
+                for d, e in call:
+                    if d == core:
+                        lands[s] = len(e)
 
     if rank is not None:
         mine = slot[core]
-        g.sync.dma_start(T.xb[:], T.x[:]).then_inc(T.sem.ldx, 16)
+        m0 = mine * NC
+        g.sync.dma_start(T.xb[:, 0:4 * U], T.x[:, 0:4 * U]).then_inc(T.sem.lda, 16)
+        g.sync.dma_start(T.xb[:, 4 * U:4 * NC], T.x[:, 4 * U:4 * NC]).then_inc(T.sem.ldb, 16)
         g.sync.dma_start(T.wb[:], T.w[:]).then_inc(T.sem.ldw, 16)
 
-        g.vector.wait_ge(T.sem.ldx, 16)
-        g.vector.quantize_mx(T.xq[:, mine * NC:(mine + 1) * NC], T.xs[:, mine * NC:(mine + 1) * NC],
-                             T.xb[:]).then_inc(T.sem.qx, 1)
+        g.vector.wait_ge(T.sem.lda, 16)
+        g.vector.quantize_mx(T.xq[:, m0:m0 + U], T.xs[:, m0:m0 + U], T.xb[:, 0:4 * U]).then_inc(T.sem.qa, 1)
+        g.vector.wait_ge(T.sem.ldb, 16)
+        g.vector.quantize_mx(T.xq[:, m0 + U:m0 + NC], T.xs[:, m0 + U:m0 + NC],
+                             T.xb[:, 4 * U:4 * NC]).then_inc(T.sem.qb, 1)
         g.vector.wait_ge(T.sem.ldw, 16)
         for j in range(N):
             g.vector.quantize_mx(T.wq[:, j * WC:(j + 1) * WC], T.ws[:, j * WC:(j + 1) * WC],
                                  T.wb[:, j * 4 * WC:(j + 1) * 4 * WC]).then_inc(T.sem.qw, 1)
-        g.wait_ge(T.sem.qx, 1)
+        g.wait_ge(T.sem.qa, 1)
 
     left = 0
-    for need, lo, n, targets in sends[core]:
-        a, b = lo * NC, (lo + n) * NC
-        for tag, ap in (("as%d", T.xs[:, a:b]), ("ac%d", T.xq[:, a:b].bitcast(dt.uint8))):
-            for s in need:
-                g.wait_ge(T.sem[tag % lands[s][0]], lands[s][1])
-            trs = []
-            for d, e in targets:
-                rid, pid, _se = topo.addr(d)
-                trs.append(RemoteDMATransfer(dst_ids=[DstId(rid=rid, pnc=pid)], dma_engine_mask=sum(1 << k for k in e),
-                                             remote_sem=T.sem[tag % lo], src=ap, dst=ap))
-                left += len(e)
-            g.remote_dma_fused(trs, local_sem=T.sem.sent)
+    whole = False
+    for need, s, calls in sends[core]:
+        a = s * NC
+        aps = (T.xq[:, a:a + U].bitcast(dt.uint8), T.xs[:, a:a + NC], T.xq[:, a + U:a + NC].bitcast(dt.uint8))
+        for i, ap in enumerate(aps):
+            if need is None and i > 0 and not whole:
+                g.wait_ge(T.sem.qb, 1)
+                whole = True
+            if need is not None:
+                g.wait_ge(T.sem[PARTS[i] % need], lands[need])
+            for call in calls:
+                trs = []
+                for d, e in call:
+                    rid, pid, _se = topo.addr(d)
+                    trs.append(RemoteDMATransfer(dst_ids=[DstId(rid=rid, pnc=pid)],
+                                                 dma_engine_mask=sum(1 << k for k in e),
+                                                 remote_sem=T.sem[PARTS[i] % s], src=ap, dst=ap))
+                    left += len(e)
+                g.remote_dma_fused(trs, local_sem=T.sem.sent)
 
     if rank is not None:
-        g.tensor.wait_ge(T.sem.qx, 1)
+        g.tensor.wait_ge(T.sem.qa, 1)
+        g.tensor.wait_ge(T.sem.qb, 1)
         g.tensor.wait_ge(T.sem.qw, N)
         for i, s in enumerate(order[core]):
-            if s != mine:
-                g.tensor.wait_ge(T.sem["as%d" % lands[s][0]], lands[s][1])
-                g.tensor.wait_ge(T.sem["ac%d" % lands[s][0]], lands[s][1])
             j = rank_in[s]
-            mmi = g.tensor.matmul_mx(T.acc[:, 0:NC], T.wq[:, j * WC:(j + 1) * WC], T.ws[:, j * WC:(j + 1) * WC],
-                                     T.xq[:, s * NC:(s + 1) * NC], T.xs[:, s * NC:(s + 1) * NC], i == 0, i == N - 1)
-        mmi.then_inc(T.sem.mm, 1)
+            a = s * NC
+            if s != mine:
+                g.tensor.wait_ge(T.sem[PARTS[0] % s], lands[s])
+                g.tensor.wait_ge(T.sem[PARTS[1] % s], lands[s])
+            mma = g.tensor.matmul_mx(T.acc[:, 0:U], T.wq[:, j * WC:(j + 1) * WC], T.ws[:, j * WC:(j + 1) * WC],
+                                     T.xq[:, a:a + U], T.xs[:, a:a + U], i == 0, i == N - 1)
+            if s != mine:
+                g.tensor.wait_ge(T.sem[PARTS[2] % s], lands[s])
+            mmb = g.tensor.matmul_mx(T.acc[:, BANK:BANK + U], T.wq[:, j * WC:(j + 1) * WC],
+                                     T.ws[:, j * WC:(j + 1) * WC],
+                                     T.xq[:, a + U:a + NC], T.xs[:, a + U:a + NC], i == 0, i == N - 1)
+            if i == N - 1:
+                mma.then_inc(T.sem.ma, 1)
+                mmb.then_inc(T.sem.mb, 1)
 
-        g.vector.wait_ge(T.sem.mm, 1)
-        g.vector.tensor_copy(T.yb[:], T.acc[:, 0:NC]).then_inc(T.sem.cp, 1)
-        g.sync.wait_ge(T.sem.cp, 1)
+        g.vector.wait_ge(T.sem.ma, 1)
+        g.vector.tensor_copy(T.yb[:, 0:U], T.acc[:, 0:U]).then_inc(T.sem.cp, 1)
+        g.vector.wait_ge(T.sem.mb, 1)
+        g.vector.tensor_copy(T.yb[:, U:NC], T.acc[:, BANK:BANK + U]).then_inc(T.sem.cp, 1)
+        g.sync.wait_ge(T.sem.cp, 2)
         g.sync.dma_start(T.y[:], T.yb[:]).then_inc(T.sem.st, 16)
         g.sync.wait_ge(T.sem.st, 16)
     g.wait_ge(T.sem.sent, left)

from concourse.bass import DstId, RemoteDMATransfer
from concourse.mybir import dt

N = 6
NC = 256
U = 128
WC = 128
BANK = 512
SIM = 112

SCRATCH = {
    "xb": ("sbuf", [128, 4 * NC], "bfloat16"),
    "wb": ("sbuf", [128, N * 4 * WC], "bfloat16"),
    "xq": ("sbuf", [128, N * NC], "float8_e4m3fn_x4"),
    "xs": ("sbuf", [128, N * NC], "uint8"),
    "wq": ("sbuf", [128, N * WC], "float8_e4m3fn_x4"),
    "ws": ("sbuf", [128, N * WC], "uint8"),
    "acc": ("psum", [128, 2 * BANK], "float32"),
    "yb": ("sbuf", [128, NC], "float32"),
}
PARTS = ("ca%d", "as%d", "cb%d")
SEMAPHORES = (["lda", "ldb", "ldw", "qa", "qb", "qw", "ma", "mb", "cp", "st", "sent"]
              + [p % k for p in PARTS for k in range(N)])


def _bits(m):
    return [e for e in range(m.bit_length()) if (m >> e) & 1]


def _plan(cores, topo):
    chips = sorted({topo.chip(c) for c in cores})
    lone = [a for a in chips if not any(topo.same_plane(a, b) for b in chips if b != a)][0]
    twins = [a for a in chips if a != lone]

    def split(ch):
        here = [c for c in cores if topo.chip(c) == ch]
        away = [c for c in cores if topo.chip(c) != ch]
        gate = [c for c in here if all(topo.may_write(c, d) for d in away)][0]
        return [c for c in here if c != gate][0], gate

    def carriers(gate, same_die):
        return [c for c in range(SIM) if c not in cores and topo.chip(c) == topo.chip(gate)
                and (topo.die(c) == topo.die(gate)) == same_die and all(topo.may_write(c, d) for d in cores)]

    pn, po = split(lone)
    qn, qo = split(twins[0])
    rn, ro = split(twins[1])
    hp, hp2 = carriers(po, False)[:2]
    hq, hr = carriers(qo, False)[0], carriers(ro, True)[0]
    slot = {pn: 0, po: 1, qn: 2, qo: 3, ro: 4, rn: 5}
    mate_of = {pn: po, po: pn, qn: qo, qo: qn, rn: ro, ro: rn, hp: po, hp2: po, hq: qo, hr: ro}

    def eng(src, key):
        wide = _bits(topo.mask(src, mate_of[src]))
        far = _bits(topo.mask(src, [c for c in cores if topo.chip(c) != topo.chip(src)][0]))
        h = len(far) // 2
        return {"wide": wide, "far": far, "far0": far[:h], "far1": far[h:],
                "near": [e for e in wide if e not in far]}[key]

    raw = {
        pn: [(None, 0, [[(hp, "near")], [(hp2, "far")]]),
             (None, 0, [[(po, "near")]]),
             (3, 3, [[(po, "wide")]]),
             (2, 2, [[(po, "wide")]])],
        hp: [(0, 0, [[(qn, "far")]])],
        hp2: [(0, 0, [[(rn, "far")]])],
        po: [(None, 1, [[(qo, "far0"), (ro, "far1")]]),
             (None, 1, [[(pn, "near")]]),
             (4, 4, [[(pn, "wide")]]),
             (5, 5, [[(pn, "wide")]])],
        qn: [(None, 2, [[(hq, "near")], [(ro, "far")]]),
             (None, 2, [[(qo, "near")]]),
             (4, 4, [[(qo, "wide")]]),
             (0, 0, [[(qo, "wide")]])],
        rn: [(None, 5, [[(hr, "near")], [(qo, "far")]]),
             (None, 5, [[(ro, "near")]]),
             (3, 3, [[(ro, "wide")]]),
             (0, 0, [[(ro, "wide")]])],
        hq: [(2, 2, [[(pn, "far")]])],
        hr: [(5, 5, [[(po, "far")]])],
        qo: [(None, 3, [[(pn, "far0"), (rn, "far1")]]),
             (None, 3, [[(qn, "near")]]),
             (5, 5, [[(qn, "wide")]]),
             (1, 1, [[(qn, "wide")]])],
        ro: [(None, 4, [[(po, "far0"), (qn, "far1")]]),
             (None, 4, [[(rn, "near")]]),
             (2, 2, [[(rn, "wide")]]),
             (1, 1, [[(rn, "wide")]])],
    }
    sends = {c: [(need, s, [[(d, eng(c, k)) for d, k in call] for call in calls])
                 for need, s, calls in raw[c]] for c in raw}
    order = {pn: (0, 1, 3, 4, 2, 5), po: (1, 0, 4, 3, 5, 2),
             qn: (2, 3, 5, 4, 0, 1), qo: (3, 2, 5, 4, 1, 0),
             rn: (5, 4, 2, 3, 0, 1), ro: (4, 5, 2, 3, 1, 0)}
    return slot, sends, order


def rank_program(g, core, T, topo):
    rank = T.rank_of(core)
    cores = list(T.cores)
    slot, sends, order = _plan(cores, topo)
    if core not in sends:
        return
    rank_in = {slot[c]: T.rank_of(c) for c in cores}

    lands = {}
    for c in sends:
        for need, s, calls in sends[c]:
            for call in calls:
                for d, e in call:
                    if d == core:
                        lands[s] = len(e)

    if rank is not None:
        mine = slot[core]
        m0 = mine * NC
        g.sync.dma_start(T.xb[:, 0:4 * U], T.x[:, 0:4 * U]).then_inc(T.sem.lda, 16)
        g.sync.dma_start(T.xb[:, 4 * U:4 * NC], T.x[:, 4 * U:4 * NC]).then_inc(T.sem.ldb, 16)
        g.sync.dma_start(T.wb[:], T.w[:]).then_inc(T.sem.ldw, 16)

        g.vector.wait_ge(T.sem.lda, 16)
        g.vector.quantize_mx(T.xq[:, m0:m0 + U], T.xs[:, m0:m0 + U], T.xb[:, 0:4 * U]).then_inc(T.sem.qa, 1)
        g.vector.wait_ge(T.sem.ldb, 16)
        g.vector.quantize_mx(T.xq[:, m0 + U:m0 + NC], T.xs[:, m0 + U:m0 + NC],
                             T.xb[:, 4 * U:4 * NC]).then_inc(T.sem.qb, 1)
        g.vector.wait_ge(T.sem.ldw, 16)
        for j in range(N):
            g.vector.quantize_mx(T.wq[:, j * WC:(j + 1) * WC], T.ws[:, j * WC:(j + 1) * WC],
                                 T.wb[:, j * 4 * WC:(j + 1) * 4 * WC]).then_inc(T.sem.qw, 1)
        g.wait_ge(T.sem.qa, 1)

    left = 0
    whole = False
    for need, s, calls in sends[core]:
        a = s * NC
        aps = (T.xq[:, a:a + U].bitcast(dt.uint8), T.xs[:, a:a + NC], T.xq[:, a + U:a + NC].bitcast(dt.uint8))
        for i, ap in enumerate(aps):
            if need is None and i > 0 and not whole:
                g.wait_ge(T.sem.qb, 1)
                whole = True
            if need is not None:
                g.wait_ge(T.sem[PARTS[i] % need], lands[need])
            for call in calls:
                trs = []
                for d, e in call:
                    rid, pid, _se = topo.addr(d)
                    trs.append(RemoteDMATransfer(dst_ids=[DstId(rid=rid, pnc=pid)],
                                                 dma_engine_mask=sum(1 << k for k in e),
                                                 remote_sem=T.sem[PARTS[i] % s], src=ap, dst=ap))
                    left += len(e)
                g.remote_dma_fused(trs, local_sem=T.sem.sent)

    if rank is not None:
        g.tensor.wait_ge(T.sem.qa, 1)
        g.tensor.wait_ge(T.sem.qb, 1)
        g.tensor.wait_ge(T.sem.qw, N)
        for i, s in enumerate(order[core]):
            j = rank_in[s]
            a = s * NC
            if s != mine:
                g.tensor.wait_ge(T.sem[PARTS[0] % s], lands[s])
                g.tensor.wait_ge(T.sem[PARTS[1] % s], lands[s])
            mma = g.tensor.matmul_mx(T.acc[:, 0:U], T.wq[:, j * WC:(j + 1) * WC], T.ws[:, j * WC:(j + 1) * WC],
                                     T.xq[:, a:a + U], T.xs[:, a:a + U], i == 0, i == N - 1)
            if s != mine:
                g.tensor.wait_ge(T.sem[PARTS[2] % s], lands[s])
            mmb = g.tensor.matmul_mx(T.acc[:, BANK:BANK + U], T.wq[:, j * WC:(j + 1) * WC],
                                     T.ws[:, j * WC:(j + 1) * WC],
                                     T.xq[:, a + U:a + NC], T.xs[:, a + U:a + NC], i == 0, i == N - 1)
            if i == N - 1:
                mma.then_inc(T.sem.ma, 1)
                mmb.then_inc(T.sem.mb, 1)

        g.vector.wait_ge(T.sem.ma, 1)
        g.vector.tensor_copy(T.yb[:, 0:U], T.acc[:, 0:U]).then_inc(T.sem.cp, 1)
        g.vector.wait_ge(T.sem.mb, 1)
        g.vector.tensor_copy(T.yb[:, U:NC], T.acc[:, BANK:BANK + U]).then_inc(T.sem.cp, 1)
        g.sync.wait_ge(T.sem.cp, 2)
        g.sync.dma_start(T.y[:], T.yb[:]).then_inc(T.sem.st, 16)
        g.sync.wait_ge(T.sem.st, 16)
    g.wait_ge(T.sem.sent, left)
